import numpy as np
import ml_dtypes


def mxq(x, axis, fmt="e4m3"):
    dtype, down = {"e4m3": (ml_dtypes.float8_e4m3fn, 7), "e5m2": (ml_dtypes.float8_e5m2, 14)}[fmt]
    v = np.moveaxis(np.asarray(x, np.float32).astype(ml_dtypes.bfloat16).astype(np.float64), axis, -1)
    blocks = v.reshape(v.shape[:-1] + (-1, 32))
    amax = np.abs(blocks).max(-1, keepdims=True)
    byte = np.maximum(np.where(amax > 0, np.frexp(amax)[1] - 1 + 127, 0) - down, 1)
    scale = np.exp2(byte - 127.0)
    codes = (blocks / scale).astype(np.float32).astype(dtype).astype(np.float64)
    return np.moveaxis((codes * scale).reshape(v.shape), -1, axis)


WIDE = False


def mx_kscale(k):
    if not WIDE:
        return np.ones(k)
    levels = np.array([10, -10, 5, -5, 0])
    if k % 512:
        return np.exp2(np.random.permutation(np.resize(levels, k // 32))).repeat(32)
    a = np.empty((k // 512, 16))
    for p in range(k // 512):
        a[p, :8] = np.random.permutation(np.resize(levels, 8))
        for g in range(8):
            far = levels[np.abs(levels - a[p, g]) >= 10]
            a[p, g + 8] = far[np.random.randint(len(far))]
    return np.exp2(a.ravel()).repeat(32)


def f64(x):
    return np.asarray(x).astype(np.float64)


def striped(idx):
    return np.tile(idx.reshape(-1, 16).T, (8, 1)).astype(np.uint16)


def unstriped(offs):
    return offs[:16].T.reshape(-1).astype(np.int64)


def pack_weight(w):
    k, n = w.shape
    w = f64(np.asarray(w, np.float32).astype(ml_dtypes.bfloat16)).reshape(k // 32, 32, n)
    amax = np.abs(w).max(1)
    byte = np.clip(np.where(amax > 0, np.frexp(amax)[1] - 1 + 127 - 7, 1), 1, 254)
    scaled = (w * np.exp2(127.0 - byte)[:, None, :]).reshape(k, n).astype(np.float32)
    words = np.ascontiguousarray(scaled.reshape(k // 512, 128, 4, n).transpose(0, 1, 3, 2)).astype(ml_dtypes.float8_e4m3fn).view(np.uint8)
    return words, np.ascontiguousarray(byte.astype(np.uint8).reshape(k // 512, 16, n))


def unpack_weight(words, scales):
    g, p, n, _ = words.shape
    vals = np.ascontiguousarray(words).view(ml_dtypes.float8_e4m3fn).astype(np.float64) * np.repeat(np.exp2(scales.astype(np.float64) - 127.0), 8, axis=1)[..., None]
    return vals.transpose(0, 1, 3, 2).reshape(g * 512, n)


K, T, S, J = 512, 1024, 512, 256


def setup_inputs():
    n = np.random.standard_normal
    s = mx_kscale(K)[:, None]
    packed_xT = pack_weight(n((K, T)) * s)
    packed_eT = pack_weight(n((K, T)) * s)
    return {
        "x_words": packed_xT[0],
        "x_scales": packed_xT[1],
        "e_words": packed_eT[0],
        "e_scales": packed_eT[1],
        "hT": (n((K, J)) / np.sqrt(K) / s).astype(np.float32),
        "gT": (n((K, J)) / np.sqrt(K) / s).astype(np.float32),
        "offs": striped(np.random.permutation(T)[:S]),
    }


def reference(x_words, x_scales, e_words, e_scales, hT, gT, offs):
    hTq = mxq(f64(hT), 0, "e4m3")
    xq = unpack_weight(x_words, x_scales)[:, unstriped(offs)]
    y = hTq.T @ xq
    e = np.exp(y - y.max(axis=1, keepdims=True))
    p = e / e.sum(axis=1, keepdims=True)
    gTq = mxq(f64(gT), 0, "e4m3")
    e_offs = unpack_weight(e_words, e_scales)[:, unstriped(offs)]
    z = gTq.T @ e_offs
    e = np.exp(z - z.max(axis=1, keepdims=True))
    q = e / e.sum(axis=1, keepdims=True)
    return np.maximum(p, q)

@@ -1,0 +1,153 @@
+from contextlib import ExitStack
+
+import concourse.mybir as mybir
+
+K, T, S, J = 512, 1024, 512, 256
+FLOPS = 2 * 2 * K * S * J
+
+F32 = mybir.dt.float32
+BF16 = mybir.dt.bfloat16
+I32 = mybir.dt.int32
+U32 = mybir.dt.uint32
+U16 = mybir.dt.uint16
+U8 = mybir.dt.uint8
+FP8X4 = mybir.dt.float8_e4m3fn_x4
+ALU = mybir.AluOpType
+ACT = mybir.ActivationFunctionType
+AXIS_X = mybir.AxisListType.X
+
+P = 128
+PACK = 4
+RUN = 4
+
+
+def tile_picked_zhyb_rrf_p_kernel(tc, x_words, x_scales, e_words, e_scales, hT, gT, offs, out):
+    nc = tc.nc
+    with ExitStack() as ctx:
+        sb = ctx.enter_context(tc.tile_pool(name="sb", bufs=1))
+        reuse = ctx.enter_context(tc.tile_pool(name="reuse", bufs=1))
+        psum = ctx.enter_context(tc.psum_pool(name="psum", bufs=1))
+
+        offsets = sb.tile([P, S // 16], U16, name="offsets")
+        x_bytes = sb.tile([P, T], U8, name="x_bytes", align_bytes=64)
+        e_bytes = sb.tile([P, T], U8, name="e_bytes", align_bytes=64)
+        x_table = sb.tile([P, T], I32, name="x_table", align_bytes=64)
+        e_table = sb.tile([P, T], I32, name="e_table", align_bytes=64)
+        h_raw = sb.tile([P, PACK, J], F32, name="h_raw", tag="h_then_ew", align_bytes=64)
+        g_raw = reuse.tile([P, PACK, J], F32, name="g_raw", offset=0)
+
+        def load_scales(tile, scales):
+            for q in range(4):
+                nc.sync.dma_start(tile[32 * q : 32 * q + 4, :].bitcast(I32), scales[0, 4 * q : 4 * q + 4, :].bitcast(I32))
+
+        def load_words(tile, words, queue):
+            queue.dma_start(tile[:], words[0].rearrange("p n t -> p (n t)").bitcast(I32))
+
+        def load_queries(tile, queries):
+            nc.sync.dma_start(tile[:], queries.rearrange("(p j) w -> p j w", j=PACK))
+
+        nc.vector.memset(x_bytes[:].bitcast(I32), 0)
+        nc.gpsimd.memset(e_bytes[:].bitcast(I32), 0)
+        load_words(x_table, x_words, nc.scalar)
+        nc.sync.dma_start(offsets[:], offs)
+        load_scales(x_bytes, x_scales)
+        load_queries(h_raw, hT)
+        load_scales(e_bytes, e_scales)
+        load_words(e_table, e_words, nc.sync)
+        load_queries(g_raw, gT)
+
+        def gather(name, table, dtype, tag):
+            picked = sb.tile([P, S], dtype, name=name, tag=tag, align_bytes=64)
+            nc.vector.tensor_copy(picked[:], table[:].bitcast(dtype).indirect(offsets[:]))
+            return picked
+
+        def gather_bytes(name, table):
+            picked = sb.tile([P, S], U8, name=name, align_bytes=64)
+            nc.vector.tensor_copy(picked[:], table[:].indirect(offsets[:]))
+            return picked
+
+        def cast(name, raw):
+            grouped = sb.tile([P, raw.shape[2] * PACK], BF16, name=name, align_bytes=64)
+            nc.scalar.activation(
+                grouped[:].rearrange("p (c i t) -> p c t i", i=RUN, t=PACK),
+                raw.rearrange("p t (c i) -> p c t i", i=RUN),
+                ACT.Copy,
+            )
+            return grouped
+
+        def quantize(name, grouped):
+            width = grouped.shape[1] // PACK
+            codes = sb.tile([P, width], U32, name=name + "_codes", align_bytes=64)
+            scales = sb.tile([P, width], U8, name=name + "_scales", align_bytes=64)
+            nc.vector.quantize_mx(out=codes[:].bitcast(FP8X4), scales=scales[:], in_=grouped[:])
+            return codes, scales
+
+        def scores(name, codes, scales, words, planes, m):
+            bank = psum.tile([P, S], F32, name=name)
+            cols = slice(m * P, (m + 1) * P)
+            nc.tensor.matmul_mx(
+                out=bank[:],
+                lhsT=codes[:, cols].bitcast(FP8X4),
+                lhsT_scale=scales[:, cols],
+                rhs=words[:].bitcast(FP8X4),
+                rhs_scale=planes[:],
+                start=True,
+                stop=True,
+            )
+            return bank
+
+        def neg_max(stat, bank):
+            nc.vector.tensor_reduce(stat, bank[:], AXIS_X, ALU.max, negate=True)
+            return stat
+
+        def exponent(name, ex, bank, shift):
+            total = sb.tile([P, 1], F32, name=name + "_sum")
+            nc.scalar.activation(ex[:], bank[:], ACT.Exp, bias=shift, scale=1.0, accum_out=total[:])
+            return ex, total
+
+        def inverse(name, total):
+            inv = sb.tile([P, 1], F32, name=name)
+            nc.vector.reciprocal(inv[:], total[:])
+            return inv
+
+        def scale(name, ex, inv):
+            p = sb.tile([P, S], F32, name=name)
+            nc.gpsimd.tensor_scalar(p[:], ex[:], inv[:], 0.0, ALU.mult, ALU.add)
+            return p
+
+        xs = gather_bytes("xs", x_bytes)
+        xw = gather("xw", x_table, U32, "xw")
+        hb = cast("hb", h_raw[:])
+        es = gather_bytes("es", e_bytes)
+        hc, hs = quantize("h", hb)
+        ew = gather("ew", e_table, U32, "h_then_ew")
+        gb = [cast(f"gb{m}", g_raw[:, :, m * P : (m + 1) * P]) for m in range(2)]
+        y = [scores(f"y{m}", hc, hs, xw, xs, m) for m in range(2)]
+
+        my0 = sb.tile([P, 1], F32, name="my0")
+        ey0 = reuse.tile([P, S], F32, name="ey0", offset=0)
+        my1 = reuse.tile([P, 1], F32, name="my1", offset=2048)
+        ey1 = sb.tile([P, S], F32, name="ey1")
+        ey0, sy0 = exponent("ey0", ey0, y[0], neg_max(my0[:], y[0]))
+        z = []
+        for m in range(2):
+            gc, gs = quantize(f"g{m}", gb[m])
+            z.append(scores(f"z{m}", gc, gs, ew, es, 0))
+        ey1, sy1 = exponent("ey1", ey1, y[1], neg_max(my1[:], y[1]))
+        p0 = scale("p0", ey0, inverse("ry0", sy0))
+        mz = sb.tile([P, 2], F32, name="mz")
+        ez = []
+        for m in range(2):
+            ex = sb.tile([P, S], F32, name=f"ez{m}")
+            ez.append(exponent(f"ez{m}", ex, z[m], neg_max(mz[:, m : m + 1], z[m])))
+        ry1 = inverse("ry1", sy1)
+        halves = ((0, S // 2), (S // 2, S))
+        p1 = sb.tile([P, S], F32, name="p1")
+        for lo, hi in halves:
+            nc.scalar.activation(p1[:, lo:hi], ey1[:, lo:hi], ACT.Copy, scale=ry1[:])
+        for m, p in enumerate((p0, p1)):
+            rz = inverse(f"rz{m}", ez[m][1])
+            res = sb.tile([P, S], F32, name=f"res{m}")
+            for lo, hi in ((0, S),) if m == 0 else halves:
+                nc.vector.scalar_tensor_tensor(res[:, lo:hi], ez[m][0][:, lo:hi], rz[:], p[:, lo:hi], ALU.mult, ALU.max)
+                nc.sync.dma_start(out[m * P : (m + 1) * P, lo:hi], res[:, lo:hi])

@@ -48,12 +48,12 @@ def tile_picked_zhyb_rrf_p_kernel(tc, x_words, x_scales, e_words, e_scales, hT, 
 
         nc.vector.memset(x_bytes[:].bitcast(I32), 0)
         nc.gpsimd.memset(e_bytes[:].bitcast(I32), 0)
-        load_words(x_table, x_words, nc.scalar)
         nc.sync.dma_start(offsets[:], offs)
+        load_words(x_table, x_words, nc.sync)
         load_scales(x_bytes, x_scales)
         load_queries(h_raw, hT)
-        load_scales(e_bytes, e_scales)
         load_words(e_table, e_words, nc.sync)
+        load_scales(e_bytes, e_scales)
         load_queries(g_raw, gT)
 
         def gather(name, table, dtype, tag):
@@ -61,8 +61,8 @@ def tile_picked_zhyb_rrf_p_kernel(tc, x_words, x_scales, e_words, e_scales, hT, 
             nc.vector.tensor_copy(picked[:], table[:].bitcast(dtype).indirect(offsets[:]))
             return picked
 
-        def gather_bytes(name, table):
-            picked = sb.tile([P, S], U8, name=name, align_bytes=64)
+        def gather_bytes(name, table, tag):
+            picked = sb.tile([P, S], U8, name=name, tag=tag, align_bytes=64)
             nc.vector.tensor_copy(picked[:], table[:].indirect(offsets[:]))
             return picked
 
@@ -78,7 +78,7 @@ def tile_picked_zhyb_rrf_p_kernel(tc, x_words, x_scales, e_words, e_scales, hT, 
         def quantize(name, grouped):
             width = grouped.shape[1] // PACK
             codes = sb.tile([P, width], U32, name=name + "_codes", align_bytes=64)
-            scales = sb.tile([P, width], U8, name=name + "_scales", align_bytes=64)
+            scales = sb.tile([P, width], U8, name=name + "_scales", tag=name + "_scales", align_bytes=64)
             nc.vector.quantize_mx(out=codes[:].bitcast(FP8X4), scales=scales[:], in_=grouped[:])
             return codes, scales
 
@@ -112,37 +112,36 @@ def tile_picked_zhyb_rrf_p_kernel(tc, x_words, x_scales, e_words, e_scales, hT, 
 
         def scale(name, ex, inv):
             p = sb.tile([P, S], F32, name=name)
-            nc.gpsimd.tensor_scalar(p[:], ex[:], inv[:], 0.0, ALU.mult, ALU.add)
+            nc.scalar.activation(p[:], ex[:], ACT.Copy, scale=inv[:])
             return p
 
-        xs = gather_bytes("xs", x_bytes)
         xw = gather("xw", x_table, U32, "xw")
+        xs = gather_bytes("xs", x_bytes, "xs")
         hb = cast("hb", h_raw[:])
-        es = gather_bytes("es", e_bytes)
         hc, hs = quantize("h", hb)
         ew = gather("ew", e_table, U32, "h_then_ew")
         gb = [cast(f"gb{m}", g_raw[:, :, m * P : (m + 1) * P]) for m in range(2)]
         y = [scores(f"y{m}", hc, hs, xw, xs, m) for m in range(2)]
-
-        my0 = sb.tile([P, 1], F32, name="my0")
+        my0 = reuse.tile([P, 16], F32, name="my0", offset=4096)
         ey0 = reuse.tile([P, S], F32, name="ey0", offset=0)
-        my1 = reuse.tile([P, 1], F32, name="my1", offset=2048)
-        ey1 = sb.tile([P, S], F32, name="ey1")
-        ey0, sy0 = exponent("ey0", ey0, y[0], neg_max(my0[:], y[0]))
+        ey0, sy0 = exponent("ey0", ey0, y[0], neg_max(my0[:, 0:1], y[0]))
+        es = gather_bytes("es", e_bytes, "h_scales")
         z = []
         for m in range(2):
             gc, gs = quantize(f"g{m}", gb[m])
             z.append(scores(f"z{m}", gc, gs, ew, es, 0))
-        ey1, sy1 = exponent("ey1", ey1, y[1], neg_max(my1[:], y[1]))
         p0 = scale("p0", ey0, inverse("ry0", sy0))
-        mz = sb.tile([P, 2], F32, name="mz")
+        my1 = reuse.tile([P, 1], F32, name="my1", offset=4096)
+        mz = reuse.tile([P, 2], F32, name="mz", offset=4096 + 32)
+        ey1 = sb.tile([P, S], F32, name="ey1")
+        ey1, sy1 = exponent("ey1", ey1, y[1], neg_max(my1[:], y[1]))
         ez = []
         for m in range(2):
             ex = sb.tile([P, S], F32, name=f"ez{m}")
             ez.append(exponent(f"ez{m}", ex, z[m], neg_max(mz[:, m : m + 1], z[m])))
         ry1 = inverse("ry1", sy1)
         halves = ((0, S // 2), (S // 2, S))
-        p1 = sb.tile([P, S], F32, name="p1")
+        p1 = reuse.tile([P, S], F32, name="p1", offset=4096 + 32)
         for lo, hi in halves:
             nc.scalar.activation(p1[:, lo:hi], ey1[:, lo:hi], ACT.Copy, scale=ry1[:])
         for m, p in enumerate((p0, p1)):

@@ -75,9 +75,9 @@ def tile_picked_zhyb_rrf_p_kernel(tc, x_words, x_scales, e_words, e_scales, hT, 
             )
             return grouped
 
-        def quantize(name, grouped):
+        def quantize(name, grouped, tag):
             width = grouped.shape[1] // PACK
-            codes = sb.tile([P, width], U32, name=name + "_codes", align_bytes=64)
+            codes = sb.tile([P, width], U32, name=name + "_codes", tag=tag, align_bytes=64)
             scales = sb.tile([P, width], U8, name=name + "_scales", tag=name + "_scales", align_bytes=64)
             nc.vector.quantize_mx(out=codes[:].bitcast(FP8X4), scales=scales[:], in_=grouped[:])
             return codes, scales
@@ -115,38 +115,51 @@ def tile_picked_zhyb_rrf_p_kernel(tc, x_words, x_scales, e_words, e_scales, hT, 
             nc.scalar.activation(p[:], ex[:], ACT.Copy, scale=inv[:])
             return p
 
+        half = S // 2
         xw = gather("xw", x_table, U32, "xw")
         xs = gather_bytes("xs", x_bytes, "xs")
-        hb = cast("hb", h_raw[:])
-        hc, hs = quantize("h", hb)
+        hb = [cast(f"hb{m}", h_raw[:, :, m * P : (m + 1) * P]) for m in range(2)]
+        hc, hs = quantize("h0", hb[0], "h_codes")
+        y0 = scores("y0", hc, hs, xw, xs, 0)
         ew = gather("ew", e_table, U32, "h_then_ew")
+        hc, hs = quantize("h1", hb[1], "h_codes")
+        y1 = scores("y1", hc, hs, xw, xs, 0)
         gb = [cast(f"gb{m}", g_raw[:, :, m * P : (m + 1) * P]) for m in range(2)]
-        y = [scores(f"y{m}", hc, hs, xw, xs, m) for m in range(2)]
-        my0 = reuse.tile([P, 16], F32, name="my0", offset=4096)
+        my0 = reuse.tile([P, 1024], F32, name="my0", offset=4096)
         ey0 = reuse.tile([P, S], F32, name="ey0", offset=0)
-        ey0, sy0 = exponent("ey0", ey0, y[0], neg_max(my0[:, 0:1], y[0]))
-        es = gather_bytes("es", e_bytes, "h_scales")
+        ey0, sy0 = exponent("ey0", ey0, y0, neg_max(my0[:, 0:1], y0))
+        es = gather_bytes("es", e_bytes, "h0_scales")
         z = []
         for m in range(2):
-            gc, gs = quantize(f"g{m}", gb[m])
+            gc, gs = quantize(f"g{m}", gb[m], f"g_codes{m}")
             z.append(scores(f"z{m}", gc, gs, ew, es, 0))
         p0 = scale("p0", ey0, inverse("ry0", sy0))
         my1 = reuse.tile([P, 1], F32, name="my1", offset=4096)
-        mz = reuse.tile([P, 2], F32, name="mz", offset=4096 + 32)
+        mz0 = reuse.tile([P, 1], F32, name="mz0", offset=4128)
+        mz1 = reuse.tile([P, 512], F32, name="mz1", offset=5152)
         ey1 = sb.tile([P, S], F32, name="ey1")
-        ey1, sy1 = exponent("ey1", ey1, y[1], neg_max(my1[:], y[1]))
-        ez = []
-        for m in range(2):
-            ex = sb.tile([P, S], F32, name=f"ez{m}")
-            ez.append(exponent(f"ez{m}", ex, z[m], neg_max(mz[:, m : m + 1], z[m])))
+        ey1, sy1 = exponent("ey1", ey1, y1, neg_max(my1[:], y1))
+        ez0 = sb.tile([P, S], F32, name="ez0")
+        ez0, sz0 = exponent("ez0", ez0, z[0], neg_max(mz0[:], z[0]))
+        ez1 = sb.tile([P, S], F32, name="ez1")
+        ez1, sz1 = exponent("ez1", ez1, z[1], neg_max(mz1[:, 0:1], z[1]))
+
+        def finish(res, m, lo, ez, rz, p):
+            nc.vector.scalar_tensor_tensor(res[:], ez[:, lo : lo + half], rz[:], p, ALU.mult, ALU.max)
+            nc.sync.dma_start(out[m * P : (m + 1) * P, lo : lo + half], res[:])
+
         ry1 = inverse("ry1", sy1)
-        halves = ((0, S // 2), (S // 2, S))
-        p1 = reuse.tile([P, S], F32, name="p1", offset=4096 + 32)
-        for lo, hi in halves:
-            nc.scalar.activation(p1[:, lo:hi], ey1[:, lo:hi], ACT.Copy, scale=ry1[:])
-        for m, p in enumerate((p0, p1)):
-            rz = inverse(f"rz{m}", ez[m][1])
-            res = sb.tile([P, S], F32, name=f"res{m}")
-            for lo, hi in ((0, S),) if m == 0 else halves:
-                nc.vector.scalar_tensor_tensor(res[:, lo:hi], ez[m][0][:, lo:hi], rz[:], p[:, lo:hi], ALU.mult, ALU.max)
-                nc.sync.dma_start(out[m * P : (m + 1) * P, lo:hi], res[:, lo:hi])
+        rz0 = inverse("rz0", sz0)
+        p1a = reuse.tile([P, half], F32, name="p1a", offset=4128)
+        nc.vector.tensor_scalar(p1a[:], ey1[:, :half], ry1[:], None, ALU.mult)
+        res0a = sb.tile([P, half], F32, name="res0a")
+        finish(res0a, 0, 0, ez0, rz0, p0[:, :half])
+        p1b = reuse.tile([P, half], F32, name="p1b", offset=5152)
+        nc.scalar.activation(p1b[:], ey1[:, half:], ACT.Copy, scale=ry1[:])
+        rz1 = inverse("rz1", sz1)
+        res0b = reuse.tile([P, half], F32, name="res0b", offset=6176)
+        finish(res0b, 0, half, ez0, rz0, p0[:, half:])
+        res1a = sb.tile([P, half], F32, name="res1a")
+        finish(res1a, 1, 0, ez1, rz1, p1a[:])
+        res1b = sb.tile([P, half], F32, name="res1b")
+        finish(res1b, 1, half, ez1, rz1, p1b[:])

from contextlib import ExitStack

import concourse.mybir as mybir

K, T, S, J = 512, 1024, 512, 256
FLOPS = 2 * 2 * K * S * J

F32 = mybir.dt.float32
BF16 = mybir.dt.bfloat16
I32 = mybir.dt.int32
U32 = mybir.dt.uint32
U16 = mybir.dt.uint16
U8 = mybir.dt.uint8
FP8X4 = mybir.dt.float8_e4m3fn_x4
ALU = mybir.AluOpType
ACT = mybir.ActivationFunctionType
AXIS_X = mybir.AxisListType.X

P = 128
PACK = 4
RUN = 4


def tile_picked_zhyb_rrf_p_kernel(tc, x_words, x_scales, e_words, e_scales, hT, gT, offs, out):
    nc = tc.nc
    with ExitStack() as ctx:
        sb = ctx.enter_context(tc.tile_pool(name="sb", bufs=1))
        reuse = ctx.enter_context(tc.tile_pool(name="reuse", bufs=1))
        psum = ctx.enter_context(tc.psum_pool(name="psum", bufs=1))

        offsets = sb.tile([P, S // 16], U16, name="offsets")
        x_bytes = sb.tile([P, T], U8, name="x_bytes", align_bytes=64)
        e_bytes = sb.tile([P, T], U8, name="e_bytes", align_bytes=64)
        x_table = sb.tile([P, T], I32, name="x_table", align_bytes=64)
        e_table = sb.tile([P, T], I32, name="e_table", align_bytes=64)
        h_raw = sb.tile([P, PACK, J], F32, name="h_raw", tag="h_then_ew", align_bytes=64)
        g_raw = reuse.tile([P, PACK, J], F32, name="g_raw", offset=0)

        def load_scales(tile, scales):
            for q in range(4):
                nc.sync.dma_start(tile[32 * q : 32 * q + 4, :].bitcast(I32), scales[0, 4 * q : 4 * q + 4, :].bitcast(I32))

        def load_words(tile, words, queue):
            queue.dma_start(tile[:], words[0].rearrange("p n t -> p (n t)").bitcast(I32))

        def load_queries(tile, queries):
            nc.sync.dma_start(tile[:], queries.rearrange("(p j) w -> p j w", j=PACK))

        nc.vector.memset(x_bytes[:].bitcast(I32), 0)
        nc.gpsimd.memset(e_bytes[:].bitcast(I32), 0)
        nc.sync.dma_start(offsets[:], offs)
        load_words(x_table, x_words, nc.sync)
        load_scales(x_bytes, x_scales)
        load_queries(h_raw, hT)
        load_words(e_table, e_words, nc.sync)
        load_scales(e_bytes, e_scales)
        load_queries(g_raw, gT)

        def gather(name, table, dtype, tag):
            picked = sb.tile([P, S], dtype, name=name, tag=tag, align_bytes=64)
            nc.vector.tensor_copy(picked[:], table[:].bitcast(dtype).indirect(offsets[:]))
            return picked

        def gather_bytes(name, table, tag):
            picked = sb.tile([P, S], U8, name=name, tag=tag, align_bytes=64)
            nc.vector.tensor_copy(picked[:], table[:].indirect(offsets[:]))
            return picked

        def cast(name, raw):
            grouped = sb.tile([P, raw.shape[2] * PACK], BF16, name=name, align_bytes=64)
            nc.scalar.activation(
                grouped[:].rearrange("p (c i t) -> p c t i", i=RUN, t=PACK),
                raw.rearrange("p t (c i) -> p c t i", i=RUN),
                ACT.Copy,
            )
            return grouped

        def quantize(name, grouped, tag):
            width = grouped.shape[1] // PACK
            codes = sb.tile([P, width], U32, name=name + "_codes", tag=tag, align_bytes=64)
            scales = sb.tile([P, width], U8, name=name + "_scales", tag=name + "_scales", align_bytes=64)
            nc.vector.quantize_mx(out=codes[:].bitcast(FP8X4), scales=scales[:], in_=grouped[:])
            return codes, scales

        def scores(name, codes, scales, words, planes, m):
            bank = psum.tile([P, S], F32, name=name)
            cols = slice(m * P, (m + 1) * P)
            nc.tensor.matmul_mx(
                out=bank[:],
                lhsT=codes[:, cols].bitcast(FP8X4),
                lhsT_scale=scales[:, cols],
                rhs=words[:].bitcast(FP8X4),
                rhs_scale=planes[:],
                start=True,
                stop=True,
            )
            return bank

        def neg_max(stat, bank):
            nc.vector.tensor_reduce(stat, bank[:], AXIS_X, ALU.max, negate=True)
            return stat

        def exponent(name, ex, bank, shift):
            total = sb.tile([P, 1], F32, name=name + "_sum")
            nc.scalar.activation(ex[:], bank[:], ACT.Exp, bias=shift, scale=1.0, accum_out=total[:])
            return ex, total

        def inverse(name, total):
            inv = sb.tile([P, 1], F32, name=name)
            nc.vector.reciprocal(inv[:], total[:])
            return inv

        def scale(name, ex, inv):
            p = sb.tile([P, S], F32, name=name)
            nc.scalar.activation(p[:], ex[:], ACT.Copy, scale=inv[:])
            return p

        half = S // 2
        xw = gather("xw", x_table, U32, "xw")
        xs = gather_bytes("xs", x_bytes, "xs")
        hb = [cast(f"hb{m}", h_raw[:, :, m * P : (m + 1) * P]) for m in range(2)]
        hc, hs = quantize("h0", hb[0], "h_codes")
        y0 = scores("y0", hc, hs, xw, xs, 0)
        ew = gather("ew", e_table, U32, "h_then_ew")
        hc, hs = quantize("h1", hb[1], "h_codes")
        y1 = scores("y1", hc, hs, xw, xs, 0)
        gb = [cast(f"gb{m}", g_raw[:, :, m * P : (m + 1) * P]) for m in range(2)]
        my0 = reuse.tile([P, 1024], F32, name="my0", offset=4096)
        ey0 = reuse.tile([P, S], F32, name="ey0", offset=0)
        ey0, sy0 = exponent("ey0", ey0, y0, neg_max(my0[:, 0:1], y0))
        es = gather_bytes("es", e_bytes, "h0_scales")
        z = []
        for m in range(2):
            gc, gs = quantize(f"g{m}", gb[m], f"g_codes{m}")
            z.append(scores(f"z{m}", gc, gs, ew, es, 0))
        p0 = scale("p0", ey0, inverse("ry0", sy0))
        my1 = reuse.tile([P, 1], F32, name="my1", offset=4096)
        mz0 = reuse.tile([P, 1], F32, name="mz0", offset=4128)
        mz1 = reuse.tile([P, 512], F32, name="mz1", offset=5152)
        ey1 = sb.tile([P, S], F32, name="ey1")
        ey1, sy1 = exponent("ey1", ey1, y1, neg_max(my1[:], y1))
        ez0 = sb.tile([P, S], F32, name="ez0")
        ez0, sz0 = exponent("ez0", ez0, z[0], neg_max(mz0[:], z[0]))
        ez1 = sb.tile([P, S], F32, name="ez1")
        ez1, sz1 = exponent("ez1", ez1, z[1], neg_max(mz1[:, 0:1], z[1]))

        def finish(res, m, lo, ez, rz, p):
            nc.vector.scalar_tensor_tensor(res[:], ez[:, lo : lo + half], rz[:], p, ALU.mult, ALU.max)
            nc.sync.dma_start(out[m * P : (m + 1) * P, lo : lo + half], res[:])

        ry1 = inverse("ry1", sy1)
        rz0 = inverse("rz0", sz0)
        p1a = reuse.tile([P, half], F32, name="p1a", offset=4128)
        nc.vector.tensor_scalar(p1a[:], ey1[:, :half], ry1[:], None, ALU.mult)
        res0a = sb.tile([P, half], F32, name="res0a")
        finish(res0a, 0, 0, ez0, rz0, p0[:, :half])
        p1b = reuse.tile([P, half], F32, name="p1b", offset=5152)
        nc.scalar.activation(p1b[:], ey1[:, half:], ACT.Copy, scale=ry1[:])
        rz1 = inverse("rz1", sz1)
        res0b = reuse.tile([P, half], F32, name="res0b", offset=6176)
        finish(res0b, 0, half, ez0, rz0, p0[:, half:])
        res1a = sb.tile([P, half], F32, name="res1a")
        finish(res1a, 1, 0, ez1, rz1, p1a[:])
        res1b = sb.tile([P, half], F32, name="res1b")
        finish(res1b, 1, half, ez1, rz1, p1b[:])
